import numpy as np
import ml_dtypes


def mxq(x, axis, fmt="e4m3"):
    dtype, down = {"e4m3": (ml_dtypes.float8_e4m3fn, 7), "e5m2": (ml_dtypes.float8_e5m2, 14)}[fmt]
    v = np.moveaxis(np.asarray(x, np.float32).astype(ml_dtypes.bfloat16).astype(np.float64), axis, -1)
    blocks = v.reshape(v.shape[:-1] + (-1, 32))
    amax = np.abs(blocks).max(-1, keepdims=True)
    byte = np.maximum(np.where(amax > 0, np.frexp(amax)[1] - 1 + 127, 0) - down, 1)
    scale = np.exp2(byte - 127.0)
    codes = (blocks / scale).astype(np.float32).astype(dtype).astype(np.float64)
    return np.moveaxis((codes * scale).reshape(v.shape), -1, axis)


WIDE = False


def mx_kscale(k):
    if not WIDE:
        return np.ones(k)
    levels = np.array([10, -10, 5, -5, 0])
    if k % 512:
        return np.exp2(np.random.permutation(np.resize(levels, k // 32))).repeat(32)
    a = np.empty((k // 512, 16))
    for p in range(k // 512):
        a[p, :8] = np.random.permutation(np.resize(levels, 8))
        for g in range(8):
            far = levels[np.abs(levels - a[p, g]) >= 10]
            a[p, g + 8] = far[np.random.randint(len(far))]
    return np.exp2(a.ravel()).repeat(32)


def f64(x):
    return np.asarray(x).astype(np.float64)


def striped(idx):
    return np.tile(idx.reshape(-1, 16).T, (8, 1)).astype(np.uint16)


def unstriped(offs):
    return offs[:16].T.reshape(-1).astype(np.int64)


E2M1 = np.array([0.0, 0.5, 1.0, 1.5, 2.0, 3.0, 4.0, 6.0, -0.0, -0.5, -1.0, -1.5, -2.0, -3.0, -4.0, -6.0])


def pack_weight(w, fmt):
    k, n = w.shape
    w = f64(np.asarray(w, np.float32).astype(ml_dtypes.bfloat16)).reshape(k // 32, 32, n)
    amax = np.abs(w).max(1)
    if fmt == "e4m3":
        byte = np.frexp(amax)[1] - 1 + 127 - 7
    else:
        mant, ex = np.frexp(amax / 6.0)
        byte = np.where(mant > 0.5, ex, ex - 1) + 127
    byte = np.clip(np.where(amax > 0, byte, 1), 1, 254)
    scaled = (w * np.exp2(127.0 - byte)[:, None, :]).reshape(k, n).astype(np.float32)
    by_word = np.ascontiguousarray(scaled.reshape(k // 512, 128, 4, n).transpose(0, 1, 3, 2))
    if fmt == "e4m3":
        words = by_word.astype(ml_dtypes.float8_e4m3fn).view(np.uint8)
    else:
        c = by_word.astype(ml_dtypes.float4_e2m1fn).view(np.uint8) & 0xF
        words = (c[..., 0::2] | (c[..., 1::2] << 4)).reshape(k // 512, 128, 2 * n)
    return np.ascontiguousarray(words), np.ascontiguousarray(byte.astype(np.uint8).reshape(k // 512, 16, n))


def unpack_weight(words, scales, fmt):
    g, _, n = scales.shape
    words = np.ascontiguousarray(words).reshape(g, 128, n, -1)
    if fmt == "e4m3":
        vals = words.view(ml_dtypes.float8_e4m3fn).astype(np.float64)
    else:
        nib = np.empty((g, 128, n, 4), np.uint8)
        nib[..., 0::2] = words & 0xF
        nib[..., 1::2] = words >> 4
        vals = E2M1[nib]
    vals = vals * np.repeat(np.exp2(scales.astype(np.float64) - 127.0), 8, axis=1)[..., None]
    return vals.transpose(0, 1, 3, 2).reshape(g * 512, n)


def gelu(v):
    return 0.5 * v * (1.0 + np.tanh(np.sqrt(2.0 / np.pi) * (v + 0.044715 * v**3)))


def striped8(idx):
    return np.concatenate([v.reshape(-1, 16).T for v in idx]).astype(np.uint16)


def unstriped8(offs):
    return np.stack([offs[16 * g:16 * g + 16].T.reshape(-1) for g in range(8)]).astype(np.int64)


def runs(v, idx8):
    k = np.arange(v.shape[0])
    return v[k[:, None], idx8[k % 512 // 64]]


K, T, S, H, P, N = 1024, 2048, 1024, 1024, 512, 512

def setup_inputs():
    n = np.random.standard_normal
    s = mx_kscale(K)[:, None]
    u = mx_kscale(H)[:, None]
    d = {}
    d["tab_words"], d["tab_scales"] = pack_weight(n((K, T)) * s, "e4m3")
    d["offs"] = striped8(np.stack([np.random.permutation(T)[:S] for _ in range(8)]))
    d["pos1"] = striped(np.random.permutation(S)[:P])
    d["pos2"] = striped(np.random.permutation(S)[:P])
    d["w1"] = (n((K, H)) / K ** 0.5 / s * u.T).astype(np.float32)
    d["floor_h"] = ((0.5 * n(H) - 0.3) * u[:, 0]).astype(np.float32)
    d["slope"] = (1.4 * np.exp(0.3 * n(H)) / u[:, 0]).astype(np.float32)
    d["gain"] = (np.exp(0.3 * n(H)) * u[:, 0]).astype(np.float32)
    d["w2_words"], d["w2_scales"] = pack_weight(n((H, N)) / H ** 0.5 / u, "e2m1")
    d["w3"] = (1.3 * n((H, N)) / H ** 0.5 / u).astype(np.float32)
    return d

def reference(tab_words, tab_scales, offs, pos1, pos2, w1, floor_h, slope, gain,
              w2_words, w2_scales, w3):
    v = runs(unpack_weight(tab_words, tab_scales, "e4m3"), unstriped8(offs))
    h = np.maximum(mxq(f64(w1), 0, "e4m3").T @ v, f64(floor_h)[:, None])
    gun = h[:, unstriped(pos1)]
    still = h[:, unstriped(pos2)]
    change = gun - still
    level = np.tanh(f64(slope)[:, None] * still) * f64(gain)[:, None]
    w2 = unpack_weight(w2_words, w2_scales, "e2m1")
    moved = w2.T @ mxq(change, 0, "e4m3")
    expected = mxq(f64(w3), 0, "e4m3").T @ mxq(level, 0, "e4m3")
    return np.abs(moved - expected)

@@ -1,0 +1,299 @@
+from contextlib import ExitStack
+
+import concourse.mybir as mybir
+
+K, T, S, H, NP, N = 1024, 2048, 1024, 1024, 512, 512
+FLOPS = 2 * K * H * S + 2 * 2 * H * N * NP
+
+F32 = mybir.dt.float32
+BF16 = mybir.dt.bfloat16
+I32 = mybir.dt.int32
+U32 = mybir.dt.uint32
+U16 = mybir.dt.uint16
+U8 = mybir.dt.uint8
+FP8X4 = mybir.dt.float8_e4m3fn_x4
+FP4X4 = mybir.dt.float4_e2m1fn_x4
+ALU = mybir.AluOpType
+ACT = mybir.ActivationFunctionType
+
+P = 128
+BANK = 512
+
+
+def tile_list_false_start_suspicion_kernel(
+    tc, tab_words, tab_scales, offs, pos1, pos2, w1, floor_h, slope, gain, w2_words, w2_scales, w3, out
+):
+    nc = tc.nc
+    with ExitStack() as ctx:
+        lists = ctx.enter_context(tc.tile_pool(name="lists", bufs=1))
+        keep = ctx.enter_context(tc.tile_pool(name="keep", bufs=1))
+        psum = ctx.enter_context(tc.psum_pool(name="psum", bufs=1))
+
+        def held(shape, dtype, name):
+            return keep.tile(shape, dtype, name=name, align_bytes=64)
+
+        def ring(shape, dtype, name, tag, bufs):
+            return keep.tile(shape, dtype, name=name, tag=tag, bufs=bufs, align_bytes=64)
+
+        def bank(i, name):
+            return psum.tile([P, BANK], F32, name=name, tag="bank%d" % (i % 8))
+
+        scale_window = ring([P, T], U8, "scale_window", "scale_window", 1)
+        v_scales = held([P, 2 * S], U8, "v_scales")
+        zero = held([P, 1], F32, "zero")
+        zero_bias = held([P, 1], F32, "zero_bias")
+        nc.vector.memset(scale_window[:].bitcast(I32), 0)
+        nc.vector.memset(zero[:], 0.0)
+        nc.vector.memset(v_scales[:].bitcast(I32), 0)
+        nc.scalar.activation(zero_bias[:], zero[:], ACT.Tanh)
+
+        offs_t = lists.tile([P, S // 16], U16, name="offs_t")
+        pos1_t = lists.tile([P, NP // 16], U16, name="pos1_t")
+        pos2_t = lists.tile([P, NP // 16], U16, name="pos2_t")
+        windows = [held([P, T], U32, "window%d" % a) for a in range(2)]
+
+        def load_window(a, pieces):
+            words = tab_words[a].rearrange("p t i -> p (t i)").bitcast(I32)
+            for x in range(pieces):
+                cols = slice(x * T // pieces, (x + 1) * T // pieces)
+                nc.sync.dma_start(out=windows[a][:, cols].bitcast(I32), in_=words[:, cols])
+
+        def load_rows(w, a, cols, name):
+            width = cols.stop - cols.start
+            raw = ring([P, 4, width], F32, name, "raw", 3)
+            nc.sync.dma_start(out=raw[:], in_=w[512 * a : 512 * (a + 1), cols].rearrange("(p i) c -> p i c", i=4))
+            return raw
+
+        def load_vector(vec, name, queue):
+            t = held([P, 2, 4], F32, name)
+            queue.dma_start(out=t[:], in_=vec.rearrange("(b p t) -> p b t", p=P, t=4))
+            return t
+
+        nc.sync.dma_start(offs_t[:], offs)
+        for a in range(2):
+            nc.sync.dma_start(out=scale_window[4 * a : P : 8, :].bitcast(I32), in_=tab_scales[a].bitcast(I32))
+        load_window(0, 1)
+        nc.sync.dma_start(pos2_t[:], pos2)
+        nc.sync.dma_start(pos1_t[:], pos1)
+        floor_t = load_vector(floor_h, "floor_t", nc.sync)
+        slope_t = load_vector(slope, "slope_t", nc.gpsimd)
+        gain_t = load_vector(gain, "gain_t", nc.gpsimd)
+        raw00 = load_rows(w1, 0, slice(0, 512), "raw00")
+        load_window(1, 1)
+        raw10 = [load_rows(w1, 1, slice(256 * u, 256 * (u + 1)), "raw10_%d" % u) for u in range(2)]
+
+        picked_scales = held([P, S], U8, "picked_scales")
+        nc.vector.tensor_copy(picked_scales[:], scale_window[:].indirect(offs_t[:]))
+        for d in range(4):
+            nc.scalar.dma_start(
+                out=v_scales[32 * d : 32 * d + 4, :].bitcast(I32),
+                in_=picked_scales[32 * d : 32 * (d + 1) : 4, :].bitcast(I32),
+            )
+        v_codes = {}
+
+        def gather_words(a):
+            for u in range(2):
+                name = "v_codes%d%d" % (a, u)
+                v_codes[a, u] = ring([P, BANK], U32, name, "scale_window" if (a, u) == (0, 1) else name, 1)
+                nc.vector.tensor_copy(v_codes[a, u][:], windows[a][:].indirect(offs_t[:, 32 * u : 32 * (u + 1)]))
+
+        def round_w1(raw, grouped, m0, on_vector, pieces):
+            ms = raw.shape[2] // 4
+            step = ms // pieces
+            for x in range(pieces):
+                src = raw[:].rearrange("p i (m t) -> p m i t", t=4)[:, x * step : (x + 1) * step]
+                dst = grouped[:].rearrange("p (t m i) -> p m i t", t=4, i=4)[:, m0 + x * step : m0 + (x + 1) * step]
+                if on_vector:
+                    nc.vector.tensor_copy(dst, src)
+                else:
+                    nc.scalar.copy(dst, src)
+
+        def quantize(grouped, name, pieces):
+            width = grouped.shape[1] // 4
+            codes = held([P, width], U32, name + "_codes")
+            scales = held([P, width], U8, name + "_scales")
+            step = width // pieces
+            for x in range(pieces):
+                cols = slice(x * step, (x + 1) * step)
+                nc.vector.quantize_mx(
+                    out=codes[:, cols].bitcast(FP8X4),
+                    scales=scales[:, cols],
+                    in_=grouped[:, 4 * x * step : 4 * (x + 1) * step],
+                )
+            return codes, scales
+
+        def quantize_w1(grouped, name, apart):
+            if apart:
+                return [quantize(grouped[:, 512 * t : 512 * (t + 1)], name + "%d" % t, 1) for t in range(4)]
+            codes, scales = quantize(grouped, name, 1)
+            return [(codes[:, P * t : P * (t + 1)], scales[:, P * t : P * (t + 1)]) for t in range(4)]
+
+        def grouped_tile(width, name):
+            return ring([P, 4 * width], BF16, name, "grouped", 4)
+
+        w1q = {}
+        gather_words(0)
+        g00 = ring([P, 2048], BF16, "g00", "early0", 1)
+        round_w1(raw00, g00, 0, False, 1)
+        gather_words(1)
+        w1q[0, 0] = quantize_w1(g00, "w1q00", False)
+        g10 = ring([P, 2048], BF16, "g10", "early1", 1)
+        round_w1(raw10[0], g10, 0, False, 1)
+        round_w1(raw10[1], g10, 64, False, 1)
+        w1q[1, 0] = quantize_w1(g10, "w1q10", True)
+        raw01 = load_rows(w1, 0, slice(512, 1024), "raw01")
+        raw11 = load_rows(w1, 1, slice(512, 1024), "raw11")
+        raw3 = [load_rows(w3, a, slice(0, N), "raw3_%d" % a) for a in range(2)]
+        w2_codes = ring([P, 2, 2 * N], U8, "w2_codes", "early0", 1)
+        w2_plane = ring([P, 2 * N], U8, "w2_plane", "early1", 1)
+        nc.vector.memset(w2_plane[:].bitcast(I32), 0)
+        nc.sync.dma_start(out=w2_codes[:].bitcast(I32), in_=w2_words.rearrange("a p n -> p a n").bitcast(I32))
+        for d in range(4):
+            nc.sync.dma_start(
+                out=w2_plane[32 * d : 32 * d + 4, :].rearrange("r (a n) -> r a n", a=2).bitcast(I32),
+                in_=w2_scales[:, 4 * d : 4 * d + 4, :].rearrange("a r n -> r a n").bitcast(I32),
+            )
+
+
+        def first_pass(acc, a, b, t, u):
+            codes, scales = w1q[a, b][t]
+            nc.tensor.matmul_mx(
+                out=acc[:],
+                lhsT=codes[:].bitcast(FP8X4),
+                lhsT_scale=scales[:],
+                rhs=v_codes[a, u][:].bitcast(FP8X4),
+                rhs_scale=v_scales[:, S * a + BANK * u : S * a + BANK * (u + 1)],
+                start=(a == 0),
+                stop=(a == 1),
+            )
+
+        h = {}
+
+        def floor_slice(accs, b, t, direct):
+            h[b, t] = held([P, S], F32, "h%d%d" % (b, t))
+            f = floor_t[:, b, t : t + 1]
+            for u in range(2):
+                dst = h[b, t][:, BANK * u : BANK * (u + 1)]
+                if direct and u == 1:
+                    nc.vector.tensor_scalar(dst, accs[u][:], f, None, ALU.max)
+                else:
+                    nc.scalar.copy(dst, accs[u][:])
+            rest = h[b, t][:, 0 : (BANK if direct else S)]
+            nc.vector.tensor_scalar(rest, rest, f, None, ALU.max)
+
+        def picked_tiles(width, name, change_tag):
+            still = held([P, 4, width], F32, "still" + name)
+            change = ring([P, 4, width], F32, "change" + name, change_tag, 1)
+            level = held([P, 4, width], BF16, "level" + name)
+            return still, change, level
+
+        def pick_still(tiles, b, t, cols):
+            lst = slice(cols.start // 16, cols.stop // 16)
+            nc.vector.tensor_copy(tiles[0][:, t, :], h[b, t][:].indirect(pos2_t[:, lst]))
+
+        def pick_change(tiles, b, t, cols):
+            lst = slice(cols.start // 16, cols.stop // 16)
+            nc.vector.tensor_tensor(tiles[1][:, t, :], h[b, t][:].indirect(pos1_t[:, lst]), tiles[0][:, t, :], ALU.subtract)
+
+        def make_level(tiles, b, t):
+            width = tiles[0].shape[2]
+            bounded = ring([P, width], F32, "bounded", "bounded", 3)
+            nc.scalar.activation(bounded[:], tiles[0][:, t, :], ACT.Tanh, bias=zero_bias[:], scale=slope_t[:, b, t : t + 1])
+            nc.scalar.activation(tiles[2][:, t, :], bounded[:], ACT.Copy, scale=gain_t[:, b, t : t + 1])
+
+        def weave(src, name, on_vector, pieces=1, scale=None, tag=None):
+            width = src.shape[2]
+            grouped = grouped_tile(width, name) if tag is None else ring([P, 4 * width], BF16, name, tag, 1)
+            step = width // 4 // pieces
+            for x in range(pieces):
+                s = src[:].rearrange("p t (c i) -> p c t i", i=4)[:, x * step : (x + 1) * step]
+                d = grouped[:].rearrange("p (c i t) -> p c t i", i=4, t=4)[:, x * step : (x + 1) * step]
+                if scale is not None:
+                    nc.scalar.activation(d, s, ACT.Copy, scale=scale)
+                elif on_vector:
+                    nc.vector.tensor_copy(d, s)
+                else:
+                    nc.scalar.copy(d, s)
+            return grouped
+
+        accs = {(t, u): bank(2 * t + u, "acc0%d%d" % (t, u)) for t in range(4) for u in range(2)}
+        for t in range(4):
+            for a in range(2):
+                for u in range(2):
+                    first_pass(accs[t, u], a, 0, t, u)
+        whole = slice(0, NP)
+        tiles0 = picked_tiles(NP, "0", "change0")
+        for t in range(4):
+            floor_slice([accs[t, 0], accs[t, 1]], 0, t, t == 0)
+            pick_still(tiles0, 0, t, whole)
+            pick_change(tiles0, 0, t, whole)
+            if t < 2:
+                g = grouped_tile(512, "g%d1" % t)
+                round_w1((raw01, raw11)[t], g, 0, False, 2)
+                w1q[t, 1] = quantize_w1(g, "w1q%d1" % t, False)
+
+        for t in range(4):
+            pair = [bank(2 * t + u, "acc1%d%d" % (t, u)) for u in range(2)]
+            for a in range(2):
+                for u in range(2):
+                    first_pass(pair[u], a, 1, t, u)
+            floor_slice(pair, 1, t, False)
+        change0 = quantize(weave(tiles0[1], "gc0", True), "change0", 1)
+        w3q = []
+        for a in range(2):
+            w3q.append(quantize(weave(raw3[a], "g3%d" % a, False, pieces=2, scale=-1.0), "w3q%d" % a, 1))
+        for t in range(4):
+            make_level(tiles0, 0, t)
+        level0 = quantize(weave(tiles0[2], "gl0", False, pieces=2, tag="late1"), "level0", 1)
+
+        def level_pass(acc, a, n, level, c0, width):
+            rows = slice(P * n, P * (n + 1))
+            nc.tensor.matmul_mx(
+                out=acc[:, 0:width],
+                lhsT=w3q[a][0][:, rows].bitcast(FP8X4),
+                lhsT_scale=w3q[a][1][:, rows],
+                rhs=level[0][:, c0 : c0 + width].bitcast(FP8X4),
+                rhs_scale=level[1][:, c0 : c0 + width],
+                start=(a == 0),
+                stop=(a == 1),
+            )
+
+        def change_passes(acc, a, n, change, c0, width):
+            for x in range(0, width, P):
+                nc.tensor.matmul_mx(
+                    out=acc[:, x : x + P],
+                    lhsT=w2_codes[:, a, 2 * P * n : 2 * P * (n + 1)].bitcast(FP4X4),
+                    lhsT_scale=w2_plane[:, N * a + P * n : N * a + P * (n + 1)],
+                    rhs=change[0][:, c0 + x : c0 + x + P].bitcast(FP8X4),
+                    rhs_scale=change[1][:, c0 + x : c0 + x + P],
+                    start=False,
+                    stop=False,
+                )
+
+        outs = {(u, n): bank(4 * u + n, "res%d%d" % (u, n)) for u in range(2) for n in range(4)}
+        for u in range(2):
+            for n in range(4):
+                level_pass(outs[u, n], 0, n, level0, 256 * u, 256)
+                change_passes(outs[u, n], 0, n, change0, 256 * u, 256)
+
+        for u in range(2):
+            cols = slice(256 * u, 256 * (u + 1))
+            tiles = picked_tiles(256, "1%d" % u, "late%d" % u)
+            for t in range(4):
+                pick_still(tiles, 1, t, cols)
+                make_level(tiles, 1, t)
+            for t in range(4):
+                pick_change(tiles, 1, t, cols)
+            change1 = quantize(weave(tiles[1], "gc1%d" % u, True), "change1%d" % u, 1)
+            level1 = quantize(weave(tiles[2], "gl1%d" % u, u == 1), "level1%d" % u, 1)
+            for n in range(4):
+                change_passes(outs[u, n], 1, n, change1, 0, 256)
+            for n in range(4):
+                level_pass(outs[u, n], 1, n, level1, 0, 256)
+            for half in range(2):
+                staged = ring([P, 2, 256], F32, "staged", "staged", 4)
+                for y in range(2):
+                    nc.scalar.activation(staged[:, y, :], outs[u, 2 * half + y][:, 0:256], ACT.Abs)
+                nc.sync.dma_start(
+                    out=out[256 * half : 256 * (half + 1), cols].rearrange("(y p) j -> p y j", p=P), in_=staged[:]
+                )

@@ -50,7 +50,7 @@ def tile_list_false_start_suspicion_kernel(
         offs_t = lists.tile([P, S // 16], U16, name="offs_t")
         pos1_t = lists.tile([P, NP // 16], U16, name="pos1_t")
         pos2_t = lists.tile([P, NP // 16], U16, name="pos2_t")
-        windows = [held([P, T], U32, "window%d" % a) for a in range(2)]
+        windows = [ring([P, T], U32, "window%d" % a, "window%d" % a, 1) for a in range(2)]
 
         def load_window(a, pieces):
             words = tab_words[a].rearrange("p t i -> p (t i)").bitcast(I32)
@@ -58,31 +58,37 @@ def tile_list_false_start_suspicion_kernel(
                 cols = slice(x * T // pieces, (x + 1) * T // pieces)
                 nc.sync.dma_start(out=windows[a][:, cols].bitcast(I32), in_=words[:, cols])
 
-        def load_rows(w, a, cols, name):
+        def load_rows(w, a, cols, name, tag="raw", bufs=3):
             width = cols.stop - cols.start
-            raw = ring([P, 4, width], F32, name, "raw", 3)
+            raw = ring([P, 4, width], F32, name, tag, bufs)
             nc.sync.dma_start(out=raw[:], in_=w[512 * a : 512 * (a + 1), cols].rearrange("(p i) c -> p i c", i=4))
             return raw
 
-        def load_vector(vec, name, queue):
-            t = held([P, 2, 4], F32, name)
-            queue.dma_start(out=t[:], in_=vec.rearrange("(b p t) -> p b t", p=P, t=4))
+        def load_vector(vec, name, tag):
+            t = ring([P, 2, 4], F32, name, tag, 1)
+            nc.sync.dma_start(out=t[:], in_=vec.rearrange("(b p t) -> p b t", p=P, t=4))
             return t
 
         nc.sync.dma_start(offs_t[:], offs)
+        nc.sync.dma_start(pos2_t[:], pos2)
+        nc.sync.dma_start(pos1_t[:], pos1)
+        floor_t = load_vector(floor_h, "floor_t", "floor_t")
+        slope_t = load_vector(slope, "slope_t", "slope_t")
         for a in range(2):
             nc.sync.dma_start(out=scale_window[4 * a : P : 8, :].bitcast(I32), in_=tab_scales[a].bitcast(I32))
         load_window(0, 1)
-        nc.sync.dma_start(pos2_t[:], pos2)
-        nc.sync.dma_start(pos1_t[:], pos1)
-        floor_t = load_vector(floor_h, "floor_t", nc.sync)
-        slope_t = load_vector(slope, "slope_t", nc.gpsimd)
-        gain_t = load_vector(gain, "gain_t", nc.gpsimd)
-        raw00 = load_rows(w1, 0, slice(0, 512), "raw00")
         load_window(1, 1)
+        raw00 = load_rows(w1, 0, slice(0, 512), "raw00")
         raw10 = [load_rows(w1, 1, slice(256 * u, 256 * (u + 1)), "raw10_%d" % u) for u in range(2)]
+        w2_plane = held([P, 2 * N], U8, "w2_plane")
+        nc.gpsimd.memset(w2_plane[:].bitcast(I32), 0)
+        for d in range(4):
+            nc.gpsimd.dma_start(
+                out=w2_plane[32 * d : 32 * d + 4, :].rearrange("r (a n) -> r a n", a=2).bitcast(I32),
+                in_=w2_scales[:, 4 * d : 4 * d + 4, :].rearrange("a r n -> r a n").bitcast(I32),
+            )
 
-        picked_scales = held([P, S], U8, "picked_scales")
+        picked_scales = ring([P, S], U8, "picked_scales", "picked", 1)
         nc.vector.tensor_copy(picked_scales[:], scale_window[:].indirect(offs_t[:]))
         for d in range(4):
             nc.scalar.dma_start(
@@ -91,26 +97,24 @@ def tile_list_false_start_suspicion_kernel(
             )
         v_codes = {}
 
-        def gather_words(a):
-            for u in range(2):
+        def gather_words(a, u):
+            if True:
                 name = "v_codes%d%d" % (a, u)
-                v_codes[a, u] = ring([P, BANK], U32, name, "scale_window" if (a, u) == (0, 1) else name, 1)
+                v_codes[a, u] = ring([P, BANK], U32, name, name, 1)
                 nc.vector.tensor_copy(v_codes[a, u][:], windows[a][:].indirect(offs_t[:, 32 * u : 32 * (u + 1)]))
 
-        def round_w1(raw, grouped, m0, on_vector, pieces):
-            ms = raw.shape[2] // 4
-            step = ms // pieces
-            for x in range(pieces):
-                src = raw[:].rearrange("p i (m t) -> p m i t", t=4)[:, x * step : (x + 1) * step]
-                dst = grouped[:].rearrange("p (t m i) -> p m i t", t=4, i=4)[:, m0 + x * step : m0 + (x + 1) * step]
-                if on_vector:
-                    nc.vector.tensor_copy(dst, src)
-                else:
-                    nc.scalar.copy(dst, src)
+        def round_w1(raw, grouped, t0, m0, on_vector):
+            ts = grouped.shape[1] // 512
+            src = raw[:].rearrange("p i (m t) -> p m i t", t=4)[:, :, :, t0 : t0 + ts]
+            dst = grouped[:].rearrange("p (t m i) -> p m i t", t=ts, i=4)[:, m0 : m0 + raw.shape[2] // 4]
+            if on_vector:
+                nc.vector.tensor_copy(dst, src)
+            else:
+                nc.scalar.copy(dst, src)
 
-        def quantize(grouped, name, pieces):
+        def quantize(grouped, name, pieces, tag=None):
             width = grouped.shape[1] // 4
-            codes = held([P, width], U32, name + "_codes")
+            codes = ring([P, width], U32, name + "_codes", tag or name, 1)
             scales = held([P, width], U8, name + "_scales")
             step = width // pieces
             for x in range(pieces):
@@ -122,38 +126,34 @@ def tile_list_false_start_suspicion_kernel(
                 )
             return codes, scales
 
-        def quantize_w1(grouped, name, apart):
+        def quantize_w1(grouped, name, apart, tag=None):
+            ts = grouped.shape[1] // 512
             if apart:
-                return [quantize(grouped[:, 512 * t : 512 * (t + 1)], name + "%d" % t, 1) for t in range(4)]
-            codes, scales = quantize(grouped, name, 1)
-            return [(codes[:, P * t : P * (t + 1)], scales[:, P * t : P * (t + 1)]) for t in range(4)]
+                return [quantize(grouped[:, 512 * t : 512 * (t + 1)], name + "%d" % t, 1) for t in range(ts)]
+            codes, scales = quantize(grouped, name, 1, tag)
+            return [(codes[:, P * t : P * (t + 1)], scales[:, P * t : P * (t + 1)]) for t in range(ts)]
 
         def grouped_tile(width, name):
             return ring([P, 4 * width], BF16, name, "grouped", 4)
 
         w1q = {}
-        gather_words(0)
-        g00 = ring([P, 2048], BF16, "g00", "early0", 1)
-        round_w1(raw00, g00, 0, False, 1)
-        gather_words(1)
-        w1q[0, 0] = quantize_w1(g00, "w1q00", False)
-        g10 = ring([P, 2048], BF16, "g10", "early1", 1)
-        round_w1(raw10[0], g10, 0, False, 1)
-        round_w1(raw10[1], g10, 64, False, 1)
-        w1q[1, 0] = quantize_w1(g10, "w1q10", True)
-        raw01 = load_rows(w1, 0, slice(512, 1024), "raw01")
-        raw11 = load_rows(w1, 1, slice(512, 1024), "raw11")
+        for a in range(2):
+            for u in range(2):
+                gather_words(a, u)
+        early = {(a, y): ring([P, 1024], BF16, "g%d0%d" % (a, y), "early%d%d" % (a, y), 1) for a in range(2) for y in range(2)}
+        for y in range(2):
+            round_w1(raw00, early[0, y], 2 * y, 0, y == 0)
+        w1q[0, 0] = quantize_w1(early[0, 0], "w1q00a", False) + quantize_w1(early[0, 1], "w1q00b", False)
+        for u in range(2):
+            for y in range(2):
+                round_w1(raw10[u], early[1, y], 2 * y, 64 * u, y == 0)
+        w1q[1, 0] = quantize_w1(early[1, 0], "w1q10a", True) + quantize_w1(early[1, 1], "w1q10b", False)
+        raw01 = load_rows(w1, 0, slice(512, 1024), "raw01", "window0", 1)
+        raw11 = load_rows(w1, 1, slice(512, 1024), "raw11", "window1", 1)
         raw3 = [load_rows(w3, a, slice(0, N), "raw3_%d" % a) for a in range(2)]
-        w2_codes = ring([P, 2, 2 * N], U8, "w2_codes", "early0", 1)
-        w2_plane = ring([P, 2 * N], U8, "w2_plane", "early1", 1)
-        nc.vector.memset(w2_plane[:].bitcast(I32), 0)
+        w2_codes = ring([P, 2, 2 * N], U8, "w2_codes", "early11", 1)
         nc.sync.dma_start(out=w2_codes[:].bitcast(I32), in_=w2_words.rearrange("a p n -> p a n").bitcast(I32))
-        for d in range(4):
-            nc.sync.dma_start(
-                out=w2_plane[32 * d : 32 * d + 4, :].rearrange("r (a n) -> r a n", a=2).bitcast(I32),
-                in_=w2_scales[:, 4 * d : 4 * d + 4, :].rearrange("a r n -> r a n").bitcast(I32),
-            )
-
+        gain_t = load_vector(gain, "gain_t", "early01")
 
         def first_pass(acc, a, b, t, u):
             codes, scales = w1q[a, b][t]
@@ -170,36 +170,42 @@ def tile_list_false_start_suspicion_kernel(
         h = {}
 
         def floor_slice(accs, b, t, direct):
-            h[b, t] = held([P, S], F32, "h%d%d" % (b, t))
+            h[b, t] = ring([P, S], F32, "h%d%d" % (b, t), "h%d%d" % (b, t), 1)
             f = floor_t[:, b, t : t + 1]
-            for u in range(2):
-                dst = h[b, t][:, BANK * u : BANK * (u + 1)]
-                if direct and u == 1:
-                    nc.vector.tensor_scalar(dst, accs[u][:], f, None, ALU.max)
-                else:
-                    nc.scalar.copy(dst, accs[u][:])
-            rest = h[b, t][:, 0 : (BANK if direct else S)]
-            nc.vector.tensor_scalar(rest, rest, f, None, ALU.max)
+            if direct:
+                for u in range(2):
+                    nc.vector.tensor_scalar(h[b, t][:, BANK * u : BANK * (u + 1)], accs[u][:], f, None, ALU.max)
+            else:
+                sums = ring([P, S], F32, "sums%d" % t, "sums%d" % t, 1)
+                for u in range(2):
+                    nc.scalar.copy(sums[:, BANK * u : BANK * (u + 1)], accs[u][:])
+                nc.vector.tensor_scalar(h[b, t][:], sums[:], f, None, ALU.max)
 
-        def picked_tiles(width, name, change_tag):
-            still = held([P, 4, width], F32, "still" + name)
-            change = ring([P, 4, width], F32, "change" + name, change_tag, 1)
-            level = held([P, 4, width], BF16, "level" + name)
-            return still, change, level
+        still = {}
 
-        def pick_still(tiles, b, t, cols):
+        def pick_still(b, t, tag=None):
+            name = "still%d%d" % (b, t)
+            if b == 0:
+                still[b, t] = ring([P, NP], F32, name, tag or name, 1)
+            nc.vector.tensor_copy(still[b, t][:], h[b, t][:].indirect(pos2_t[:]))
+
+        def pick_change(change, b, t, cols):
             lst = slice(cols.start // 16, cols.stop // 16)
-            nc.vector.tensor_copy(tiles[0][:, t, :], h[b, t][:].indirect(pos2_t[:, lst]))
+            nc.vector.tensor_tensor(
+                change[:, t, :], h[b, t][:].indirect(pos1_t[:, lst]), still[b, t][:, cols], ALU.subtract
+            )
 
-        def pick_change(tiles, b, t, cols):
-            lst = slice(cols.start // 16, cols.stop // 16)
-            nc.vector.tensor_tensor(tiles[1][:, t, :], h[b, t][:].indirect(pos1_t[:, lst]), tiles[0][:, t, :], ALU.subtract)
-
-        def make_level(tiles, b, t):
-            width = tiles[0].shape[2]
-            bounded = ring([P, width], F32, "bounded", "bounded", 3)
-            nc.scalar.activation(bounded[:], tiles[0][:, t, :], ACT.Tanh, bias=zero_bias[:], scale=slope_t[:, b, t : t + 1])
-            nc.scalar.activation(tiles[2][:, t, :], bounded[:], ACT.Copy, scale=gain_t[:, b, t : t + 1])
+        def make_level(b, cols, name, last_tag="bounded"):
+            width = cols.stop - cols.start
+            level = ring([P, 4, width], BF16, name, name, 1)
+            for t in range(4):
+                tag = last_tag if t == 3 else "bounded"
+                bounded = ring([P, width], F32, "bounded", tag, 3 if tag == "bounded" else 1)
+                nc.scalar.activation(
+                    bounded[:], still[b, t][:, cols], ACT.Tanh, bias=zero_bias[:], scale=slope_t[:, b, t : t + 1]
+                )
+                nc.scalar.activation(level[:, t, :], bounded[:], ACT.Copy, scale=gain_t[:, b, t : t + 1])
+            return level
 
         def weave(src, name, on_vector, pieces=1, scale=None, tag=None):
             width = src.shape[2]
@@ -222,15 +228,22 @@ def tile_list_false_start_suspicion_kernel(
                 for u in range(2):
                     first_pass(accs[t, u], a, 0, t, u)
         whole = slice(0, NP)
-        tiles0 = picked_tiles(NP, "0", "change0")
+        late = [ring([P, 2048], BF16, "g%d1" % a, "g%d1" % a, 1) for a in range(2)]
+        for a in range(2):
+            round_w1((raw01, raw11)[a], late[a], 0, 0, False)
+        floor_slice([accs[0, 0], accs[0, 1]], 0, 0, True)
+        change_rows0 = ring([P, 4, NP], F32, "change_rows0", "change_rows0", 1)
         for t in range(4):
-            floor_slice([accs[t, 0], accs[t, 1]], 0, t, t == 0)
-            pick_still(tiles0, 0, t, whole)
-            pick_change(tiles0, 0, t, whole)
-            if t < 2:
-                g = grouped_tile(512, "g%d1" % t)
-                round_w1((raw01, raw11)[t], g, 0, False, 2)
-                w1q[t, 1] = quantize_w1(g, "w1q%d1" % t, False)
+            if t == 1:
+                for a in range(2):
+                    w1q[a, 1] = quantize_w1(late[a], "w1q%d1" % a, False, ("h00", None)[a])
+            pick_still(0, t, "g11" if t == 1 else None)
+            if t < 3:
+                floor_slice([accs[t + 1, 0], accs[t + 1, 1]], 0, t + 1, True)
+            pick_change(change_rows0, 0, t, whole)
+        w3q = []
+        for a in range(2):
+            w3q.append(quantize(weave(raw3[a], "g3%d" % a, False, pieces=1, scale=-1.0), "w3q%d" % a, 1))
 
         for t in range(4):
             pair = [bank(2 * t + u, "acc1%d%d" % (t, u)) for u in range(2)]
@@ -238,13 +251,13 @@ def tile_list_false_start_suspicion_kernel(
                 for u in range(2):
                     first_pass(pair[u], a, 1, t, u)
             floor_slice(pair, 1, t, False)
-        change0 = quantize(weave(tiles0[1], "gc0", True), "change0", 1)
-        w3q = []
-        for a in range(2):
-            w3q.append(quantize(weave(raw3[a], "g3%d" % a, False, pieces=2, scale=-1.0), "w3q%d" % a, 1))
+        still1 = ring([P, 4, NP], F32, "still1", "sums3", 1)
         for t in range(4):
-            make_level(tiles0, 0, t)
-        level0 = quantize(weave(tiles0[2], "gl0", False, pieces=2, tag="late1"), "level0", 1)
+            still[1, t] = still1[:, t, :]
+            pick_still(1, t)
+        level_rows0 = make_level(0, whole, "level_rows0")
+        change0 = quantize(weave(change_rows0, "gc0", False), "changeq0", 1)
+        level0 = quantize(weave(level_rows0, "gl0", False, tag="gl0"), "levelq0", 1)
 
         def level_pass(acc, a, n, level, c0, width):
             rows = slice(P * n, P * (n + 1))
@@ -274,26 +287,38 @@ def tile_list_false_start_suspicion_kernel(
         for u in range(2):
             for n in range(4):
                 level_pass(outs[u, n], 0, n, level0, 256 * u, 256)
+        for u in range(2):
+            for n in range(4):
                 change_passes(outs[u, n], 0, n, change0, 256 * u, 256)
+
+        def finish(u, pieces):
+            tiles_each = 4 // pieces
+            for x in range(pieces):
+                tag = "staged" if u == 0 else "staged%d" % x
+                staged = ring([P, tiles_each, 256], F32, "staged", tag, 1)
+                for y in range(tiles_each):
+                    nc.scalar.activation(staged[:, y, :], outs[u, tiles_each * x + y][:, 0:256], ACT.Abs)
+                rows = slice(P * tiles_each * x, P * tiles_each * (x + 1))
+                nc.sync.dma_start(
+                    out=out[rows, 256 * u : 256 * (u + 1)].rearrange("(y p) j -> p y j", p=P), in_=staged[:]
+                )
 
         for u in range(2):
             cols = slice(256 * u, 256 * (u + 1))
-            tiles = picked_tiles(256, "1%d" % u, "late%d" % u)
+            level_rows = make_level(1, cols, "level_rows1%d" % u, ("bounded", "staged")[u])
+            change_rows = ring([P, 4, 256], F32, "change_rows1%d" % u, ("change_rows0", "gl0")[u], 1)
             for t in range(4):
-                pick_still(tiles, 1, t, cols)
-                make_level(tiles, 1, t)
-            for t in range(4):
-                pick_change(tiles, 1, t, cols)
-            change1 = quantize(weave(tiles[1], "gc1%d" % u, True), "change1%d" % u, 1)
-            level1 = quantize(weave(tiles[2], "gl1%d" % u, u == 1), "level1%d" % u, 1)
+                pick_change(change_rows, 1, t, cols)
+            if u == 0:
+                level1 = quantize(weave(level_rows, "gl10", False), "levelq10", 1)
+                change1 = quantize(weave(change_rows, "gc10", True, tag="level_rows0"), "changeq10", 1)
+            else:
+                woven = weave(change_rows, "gc11", True, tag="level_rows10"), weave(level_rows, "gl11", True)
+                change1 = quantize(woven[0], "changeq11", 1)
+                level1 = quantize(woven[1], "levelq11", 1)
             for n in range(4):
                 change_passes(outs[u, n], 1, n, change1, 0, 256)
             for n in range(4):
                 level_pass(outs[u, n], 1, n, level1, 0, 256)
-            for half in range(2):
-                staged = ring([P, 2, 256], F32, "staged", "staged", 4)
-                for y in range(2):
-                    nc.scalar.activation(staged[:, y, :], outs[u, 2 * half + y][:, 0:256], ACT.Abs)
-                nc.sync.dma_start(
-                    out=out[256 * half : 256 * (half + 1), cols].rearrange("(y p) j -> p y j", p=P), in_=staged[:]
-                )
+        finish(0, 1)
+        finish(1, 2)

@@ -74,19 +74,13 @@ def tile_list_false_start_suspicion_kernel(
         nc.sync.dma_start(pos1_t[:], pos1)
         floor_t = load_vector(floor_h, "floor_t", "floor_t")
         slope_t = load_vector(slope, "slope_t", "slope_t")
-        for a in range(2):
-            nc.sync.dma_start(out=scale_window[4 * a : P : 8, :].bitcast(I32), in_=tab_scales[a].bitcast(I32))
+        nc.sync.dma_start(
+            out=scale_window[0:P:4, :].bitcast(I32), in_=tab_scales.rearrange("a q t -> q a t").bitcast(I32)
+        )
         load_window(0, 1)
         load_window(1, 1)
         raw00 = load_rows(w1, 0, slice(0, 512), "raw00")
         raw10 = [load_rows(w1, 1, slice(256 * u, 256 * (u + 1)), "raw10_%d" % u) for u in range(2)]
-        w2_plane = held([P, 2 * N], U8, "w2_plane")
-        nc.gpsimd.memset(w2_plane[:].bitcast(I32), 0)
-        for d in range(4):
-            nc.gpsimd.dma_start(
-                out=w2_plane[32 * d : 32 * d + 4, :].rearrange("r (a n) -> r a n", a=2).bitcast(I32),
-                in_=w2_scales[:, 4 * d : 4 * d + 4, :].rearrange("a r n -> r a n").bitcast(I32),
-            )
 
         picked_scales = ring([P, S], U8, "picked_scales", "picked", 1)
         nc.vector.tensor_copy(picked_scales[:], scale_window[:].indirect(offs_t[:]))
@@ -96,11 +90,12 @@ def tile_list_false_start_suspicion_kernel(
                 in_=picked_scales[32 * d : 32 * (d + 1) : 4, :].bitcast(I32),
             )
         v_codes = {}
+        v_words = ring([P, 4 * BANK], U32, "v_words", "v_words", 1)
 
         def gather_words(a, u):
             if True:
                 name = "v_codes%d%d" % (a, u)
-                v_codes[a, u] = ring([P, BANK], U32, name, name, 1)
+                v_codes[a, u] = v_words[:, BANK * (2 * a + u) : BANK * (2 * a + u + 1)]
                 nc.vector.tensor_copy(v_codes[a, u][:], windows[a][:].indirect(offs_t[:, 32 * u : 32 * (u + 1)]))
 
         def round_w1(raw, grouped, t0, m0, on_vector):
@@ -143,17 +138,27 @@ def tile_list_false_start_suspicion_kernel(
         early = {(a, y): ring([P, 1024], BF16, "g%d0%d" % (a, y), "early%d%d" % (a, y), 1) for a in range(2) for y in range(2)}
         for y in range(2):
             round_w1(raw00, early[0, y], 2 * y, 0, y == 0)
-        w1q[0, 0] = quantize_w1(early[0, 0], "w1q00a", False) + quantize_w1(early[0, 1], "w1q00b", False)
+        w1q[0, 0] = quantize_w1(early[0, 0], "w1q00a", False)
         for u in range(2):
             for y in range(2):
                 round_w1(raw10[u], early[1, y], 2 * y, 64 * u, y == 0)
-        w1q[1, 0] = quantize_w1(early[1, 0], "w1q10a", True) + quantize_w1(early[1, 1], "w1q10b", False)
+        w1q[1, 0] = quantize_w1(early[1, 0], "w1q10a", True)
+        w1q[0, 0] = w1q[0, 0] + quantize_w1(early[0, 1], "w1q00b", False, "early10")
+        w1q[1, 0] = w1q[1, 0] + quantize_w1(early[1, 1], "w1q10b", False)
         raw01 = load_rows(w1, 0, slice(512, 1024), "raw01", "window0", 1)
         raw11 = load_rows(w1, 1, slice(512, 1024), "raw11", "window1", 1)
         raw3 = [load_rows(w3, a, slice(0, N), "raw3_%d" % a) for a in range(2)]
         w2_codes = ring([P, 2, 2 * N], U8, "w2_codes", "early11", 1)
         nc.sync.dma_start(out=w2_codes[:].bitcast(I32), in_=w2_words.rearrange("a p n -> p a n").bitcast(I32))
         gain_t = load_vector(gain, "gain_t", "early01")
+        w2_plane = ring([P, 2 * N], U8, "w2_plane", "early00", 1)
+        nc.vector.memset(w2_plane[:].bitcast(I32), 0)
+        for d in range(4):
+            nc.sync.dma_start(
+                out=w2_plane[32 * d : 32 * d + 4, :].rearrange("r (a n) -> r a n", a=2).bitcast(I32),
+                in_=w2_scales[:, 4 * d : 4 * d + 4, :].rearrange("a r n -> r a n").bitcast(I32),
+            )
+
 
         def first_pass(acc, a, b, t, u):
             codes, scales = w1q[a, b][t]
@@ -321,4 +326,4 @@ def tile_list_false_start_suspicion_kernel(
             for n in range(4):
                 level_pass(outs[u, n], 1, n, level1, 0, 256)
         finish(0, 1)
-        finish(1, 2)
+        finish(1, 4)

@@ -150,9 +150,9 @@ def tile_list_false_start_suspicion_kernel(
         raw3 = [load_rows(w3, a, slice(0, N), "raw3_%d" % a) for a in range(2)]
         w2_codes = ring([P, 2, 2 * N], U8, "w2_codes", "early11", 1)
         nc.sync.dma_start(out=w2_codes[:].bitcast(I32), in_=w2_words.rearrange("a p n -> p a n").bitcast(I32))
-        gain_t = load_vector(gain, "gain_t", "early01")
-        w2_plane = ring([P, 2 * N], U8, "w2_plane", "early00", 1)
-        nc.vector.memset(w2_plane[:].bitcast(I32), 0)
+        gain_t = load_vector(gain, "gain_t", "early00")
+        w2_plane = ring([P, 2 * N], U8, "w2_plane", "early01", 1)
+        nc.gpsimd.memset(w2_plane[:].bitcast(I32), 0)
         for d in range(4):
             nc.sync.dma_start(
                 out=w2_plane[32 * d : 32 * d + 4, :].rearrange("r (a n) -> r a n", a=2).bitcast(I32),
@@ -181,7 +181,13 @@ def tile_list_false_start_suspicion_kernel(
                 for u in range(2):
                     nc.vector.tensor_scalar(h[b, t][:, BANK * u : BANK * (u + 1)], accs[u][:], f, None, ALU.max)
             else:
-                sums = ring([P, S], F32, "sums%d" % t, "sums%d" % t, 1)
+                if (b, t) == (1, 3):
+                    for u in range(2):
+                        sums = ring([P, BANK], F32, "last_sums%d" % u, "last_sums%d" % u, 1)
+                        nc.scalar.copy(sums[:], accs[u][:])
+                        nc.vector.tensor_scalar(h[b, t][:, BANK * u : BANK * (u + 1)], sums[:], f, None, ALU.max)
+                    return
+                sums = ring([P, S], F32, "sums%d%d" % (b, t), "sums%d" % t, 1)
                 for u in range(2):
                     nc.scalar.copy(sums[:, BANK * u : BANK * (u + 1)], accs[u][:])
                 nc.vector.tensor_scalar(h[b, t][:], sums[:], f, None, ALU.max)
@@ -202,14 +208,19 @@ def tile_list_false_start_suspicion_kernel(
 
         def make_level(b, cols, name, last_tag="bounded"):
             width = cols.stop - cols.start
-            level = ring([P, 4, width], BF16, name, name, 1)
+            level = ring([P, 4, width], BF16, name, "last_sums0" if b == 0 else name, 1)
             for t in range(4):
                 tag = last_tag if t == 3 else "bounded"
+                if b == 0:
+                    tag = "bounded%d" % t
                 bounded = ring([P, width], F32, "bounded", tag, 3 if tag == "bounded" else 1)
                 nc.scalar.activation(
                     bounded[:], still[b, t][:, cols], ACT.Tanh, bias=zero_bias[:], scale=slope_t[:, b, t : t + 1]
                 )
-                nc.scalar.activation(level[:, t, :], bounded[:], ACT.Copy, scale=gain_t[:, b, t : t + 1])
+                if b == 0:
+                    nc.gpsimd.tensor_scalar(level[:, t, :], bounded[:], gain_t[:, b, t : t + 1], 0.0, ALU.mult, ALU.add)
+                else:
+                    nc.scalar.activation(level[:, t, :], bounded[:], ACT.Copy, scale=gain_t[:, b, t : t + 1])
             return level
 
         def weave(src, name, on_vector, pieces=1, scale=None, tag=None):
@@ -244,8 +255,9 @@ def tile_list_false_start_suspicion_kernel(
                     w1q[a, 1] = quantize_w1(late[a], "w1q%d1" % a, False, ("h00", None)[a])
             pick_still(0, t, "g11" if t == 1 else None)
             if t < 3:
-                floor_slice([accs[t + 1, 0], accs[t + 1, 1]], 0, t + 1, True)
+                floor_slice([accs[t + 1, 0], accs[t + 1, 1]], 0, t + 1, t + 1 < 3)
             pick_change(change_rows0, 0, t, whole)
+
         w3q = []
         for a in range(2):
             w3q.append(quantize(weave(raw3[a], "g3%d" % a, False, pieces=1, scale=-1.0), "w3q%d" % a, 1))
@@ -256,7 +268,7 @@ def tile_list_false_start_suspicion_kernel(
                 for u in range(2):
                     first_pass(pair[u], a, 1, t, u)
             floor_slice(pair, 1, t, False)
-        still1 = ring([P, 4, NP], F32, "still1", "sums3", 1)
+        still1 = ring([P, 4, NP], F32, "still1", "last_sums1", 1)
         for t in range(4):
             still[1, t] = still1[:, t, :]
             pick_still(1, t)
@@ -299,7 +311,7 @@ def tile_list_false_start_suspicion_kernel(
         def finish(u, pieces):
             tiles_each = 4 // pieces
             for x in range(pieces):
-                tag = "staged" if u == 0 else "staged%d" % x
+                tag = "level_rows11" if u == 0 else "staged%d" % x
                 staged = ring([P, tiles_each, 256], F32, "staged", tag, 1)
                 for y in range(tiles_each):
                     nc.scalar.activation(staged[:, y, :], outs[u, tiles_each * x + y][:, 0:256], ACT.Abs)
@@ -310,15 +322,15 @@ def tile_list_false_start_suspicion_kernel(
 
         for u in range(2):
             cols = slice(256 * u, 256 * (u + 1))
-            level_rows = make_level(1, cols, "level_rows1%d" % u, ("bounded", "staged")[u])
+            level_rows = make_level(1, cols, "level_rows1%d" % u, "bounded")
             change_rows = ring([P, 4, 256], F32, "change_rows1%d" % u, ("change_rows0", "gl0")[u], 1)
             for t in range(4):
                 pick_change(change_rows, 1, t, cols)
             if u == 0:
                 level1 = quantize(weave(level_rows, "gl10", False), "levelq10", 1)
-                change1 = quantize(weave(change_rows, "gc10", True, tag="level_rows0"), "changeq10", 1)
+                change1 = quantize(weave(change_rows, "gc10", True, tag="last_sums0"), "changeq10", 1)
             else:
-                woven = weave(change_rows, "gc11", True, tag="level_rows10"), weave(level_rows, "gl11", True)
+                woven = weave(change_rows, "gc11", True, tag="level_rows10"), weave(level_rows, "gl11", False)
                 change1 = quantize(woven[0], "changeq11", 1)
                 level1 = quantize(woven[1], "levelq11", 1)
             for n in range(4):

from contextlib import ExitStack

import concourse.mybir as mybir

K, T, S, H, NP, N = 1024, 2048, 1024, 1024, 512, 512
FLOPS = 2 * K * H * S + 2 * 2 * H * N * NP

F32 = mybir.dt.float32
BF16 = mybir.dt.bfloat16
I32 = mybir.dt.int32
U32 = mybir.dt.uint32
U16 = mybir.dt.uint16
U8 = mybir.dt.uint8
FP8X4 = mybir.dt.float8_e4m3fn_x4
FP4X4 = mybir.dt.float4_e2m1fn_x4
ALU = mybir.AluOpType
ACT = mybir.ActivationFunctionType

P = 128
BANK = 512


def tile_list_false_start_suspicion_kernel(
    tc, tab_words, tab_scales, offs, pos1, pos2, w1, floor_h, slope, gain, w2_words, w2_scales, w3, out
):
    nc = tc.nc
    with ExitStack() as ctx:
        lists = ctx.enter_context(tc.tile_pool(name="lists", bufs=1))
        keep = ctx.enter_context(tc.tile_pool(name="keep", bufs=1))
        psum = ctx.enter_context(tc.psum_pool(name="psum", bufs=1))

        def held(shape, dtype, name):
            return keep.tile(shape, dtype, name=name, align_bytes=64)

        def ring(shape, dtype, name, tag, bufs):
            return keep.tile(shape, dtype, name=name, tag=tag, bufs=bufs, align_bytes=64)

        def bank(i, name):
            return psum.tile([P, BANK], F32, name=name, tag="bank%d" % (i % 8))

        scale_window = ring([P, T], U8, "scale_window", "scale_window", 1)
        v_scales = held([P, 2 * S], U8, "v_scales")
        zero = held([P, 1], F32, "zero")
        zero_bias = held([P, 1], F32, "zero_bias")
        nc.vector.memset(scale_window[:].bitcast(I32), 0)
        nc.vector.memset(zero[:], 0.0)
        nc.vector.memset(v_scales[:].bitcast(I32), 0)
        nc.scalar.activation(zero_bias[:], zero[:], ACT.Tanh)

        offs_t = lists.tile([P, S // 16], U16, name="offs_t")
        pos1_t = lists.tile([P, NP // 16], U16, name="pos1_t")
        pos2_t = lists.tile([P, NP // 16], U16, name="pos2_t")
        windows = [ring([P, T], U32, "window%d" % a, "window%d" % a, 1) for a in range(2)]

        def load_window(a, pieces):
            words = tab_words[a].rearrange("p t i -> p (t i)").bitcast(I32)
            for x in range(pieces):
                cols = slice(x * T // pieces, (x + 1) * T // pieces)
                nc.sync.dma_start(out=windows[a][:, cols].bitcast(I32), in_=words[:, cols])

        def load_rows(w, a, cols, name, tag="raw", bufs=3):
            width = cols.stop - cols.start
            raw = ring([P, 4, width], F32, name, tag, bufs)
            nc.sync.dma_start(out=raw[:], in_=w[512 * a : 512 * (a + 1), cols].rearrange("(p i) c -> p i c", i=4))
            return raw

        def load_vector(vec, name, tag):
            t = ring([P, 2, 4], F32, name, tag, 1)
            nc.sync.dma_start(out=t[:], in_=vec.rearrange("(b p t) -> p b t", p=P, t=4))
            return t

        nc.sync.dma_start(offs_t[:], offs)
        nc.sync.dma_start(pos2_t[:], pos2)
        nc.sync.dma_start(pos1_t[:], pos1)
        floor_t = load_vector(floor_h, "floor_t", "floor_t")
        slope_t = load_vector(slope, "slope_t", "slope_t")
        nc.sync.dma_start(
            out=scale_window[0:P:4, :].bitcast(I32), in_=tab_scales.rearrange("a q t -> q a t").bitcast(I32)
        )
        load_window(0, 1)
        load_window(1, 1)
        raw00 = load_rows(w1, 0, slice(0, 512), "raw00")
        raw10 = [load_rows(w1, 1, slice(256 * u, 256 * (u + 1)), "raw10_%d" % u) for u in range(2)]

        picked_scales = ring([P, S], U8, "picked_scales", "picked", 1)
        nc.vector.tensor_copy(picked_scales[:], scale_window[:].indirect(offs_t[:]))
        for d in range(4):
            nc.scalar.dma_start(
                out=v_scales[32 * d : 32 * d + 4, :].bitcast(I32),
                in_=picked_scales[32 * d : 32 * (d + 1) : 4, :].bitcast(I32),
            )
        v_codes = {}
        v_words = ring([P, 4 * BANK], U32, "v_words", "v_words", 1)

        def gather_words(a, u):
            if True:
                name = "v_codes%d%d" % (a, u)
                v_codes[a, u] = v_words[:, BANK * (2 * a + u) : BANK * (2 * a + u + 1)]
                nc.vector.tensor_copy(v_codes[a, u][:], windows[a][:].indirect(offs_t[:, 32 * u : 32 * (u + 1)]))

        def round_w1(raw, grouped, t0, m0, on_vector):
            ts = grouped.shape[1] // 512
            src = raw[:].rearrange("p i (m t) -> p m i t", t=4)[:, :, :, t0 : t0 + ts]
            dst = grouped[:].rearrange("p (t m i) -> p m i t", t=ts, i=4)[:, m0 : m0 + raw.shape[2] // 4]
            if on_vector:
                nc.vector.tensor_copy(dst, src)
            else:
                nc.scalar.copy(dst, src)

        def quantize(grouped, name, pieces, tag=None):
            width = grouped.shape[1] // 4
            codes = ring([P, width], U32, name + "_codes", tag or name, 1)
            scales = held([P, width], U8, name + "_scales")
            step = width // pieces
            for x in range(pieces):
                cols = slice(x * step, (x + 1) * step)
                nc.vector.quantize_mx(
                    out=codes[:, cols].bitcast(FP8X4),
                    scales=scales[:, cols],
                    in_=grouped[:, 4 * x * step : 4 * (x + 1) * step],
                )
            return codes, scales

        def quantize_w1(grouped, name, apart, tag=None):
            ts = grouped.shape[1] // 512
            if apart:
                return [quantize(grouped[:, 512 * t : 512 * (t + 1)], name + "%d" % t, 1) for t in range(ts)]
            codes, scales = quantize(grouped, name, 1, tag)
            return [(codes[:, P * t : P * (t + 1)], scales[:, P * t : P * (t + 1)]) for t in range(ts)]

        def grouped_tile(width, name):
            return ring([P, 4 * width], BF16, name, "grouped", 4)

        w1q = {}
        for a in range(2):
            for u in range(2):
                gather_words(a, u)
        early = {(a, y): ring([P, 1024], BF16, "g%d0%d" % (a, y), "early%d%d" % (a, y), 1) for a in range(2) for y in range(2)}
        for y in range(2):
            round_w1(raw00, early[0, y], 2 * y, 0, y == 0)
        w1q[0, 0] = quantize_w1(early[0, 0], "w1q00a", False)
        for u in range(2):
            for y in range(2):
                round_w1(raw10[u], early[1, y], 2 * y, 64 * u, y == 0)
        w1q[1, 0] = quantize_w1(early[1, 0], "w1q10a", True)
        w1q[0, 0] = w1q[0, 0] + quantize_w1(early[0, 1], "w1q00b", False, "early10")
        w1q[1, 0] = w1q[1, 0] + quantize_w1(early[1, 1], "w1q10b", False)
        raw01 = load_rows(w1, 0, slice(512, 1024), "raw01", "window0", 1)
        raw11 = load_rows(w1, 1, slice(512, 1024), "raw11", "window1", 1)
        raw3 = [load_rows(w3, a, slice(0, N), "raw3_%d" % a) for a in range(2)]
        w2_codes = ring([P, 2, 2 * N], U8, "w2_codes", "early11", 1)
        nc.sync.dma_start(out=w2_codes[:].bitcast(I32), in_=w2_words.rearrange("a p n -> p a n").bitcast(I32))
        gain_t = load_vector(gain, "gain_t", "early00")
        w2_plane = ring([P, 2 * N], U8, "w2_plane", "early01", 1)
        nc.gpsimd.memset(w2_plane[:].bitcast(I32), 0)
        for d in range(4):
            nc.sync.dma_start(
                out=w2_plane[32 * d : 32 * d + 4, :].rearrange("r (a n) -> r a n", a=2).bitcast(I32),
                in_=w2_scales[:, 4 * d : 4 * d + 4, :].rearrange("a r n -> r a n").bitcast(I32),
            )


        def first_pass(acc, a, b, t, u):
            codes, scales = w1q[a, b][t]
            nc.tensor.matmul_mx(
                out=acc[:],
                lhsT=codes[:].bitcast(FP8X4),
                lhsT_scale=scales[:],
                rhs=v_codes[a, u][:].bitcast(FP8X4),
                rhs_scale=v_scales[:, S * a + BANK * u : S * a + BANK * (u + 1)],
                start=(a == 0),
                stop=(a == 1),
            )

        h = {}

        def floor_slice(accs, b, t, direct):
            h[b, t] = ring([P, S], F32, "h%d%d" % (b, t), "h%d%d" % (b, t), 1)
            f = floor_t[:, b, t : t + 1]
            if direct:
                for u in range(2):
                    nc.vector.tensor_scalar(h[b, t][:, BANK * u : BANK * (u + 1)], accs[u][:], f, None, ALU.max)
            else:
                if (b, t) == (1, 3):
                    for u in range(2):
                        sums = ring([P, BANK], F32, "last_sums%d" % u, "last_sums%d" % u, 1)
                        nc.scalar.copy(sums[:], accs[u][:])
                        nc.vector.tensor_scalar(h[b, t][:, BANK * u : BANK * (u + 1)], sums[:], f, None, ALU.max)
                    return
                sums = ring([P, S], F32, "sums%d%d" % (b, t), "sums%d" % t, 1)
                for u in range(2):
                    nc.scalar.copy(sums[:, BANK * u : BANK * (u + 1)], accs[u][:])
                nc.vector.tensor_scalar(h[b, t][:], sums[:], f, None, ALU.max)

        still = {}

        def pick_still(b, t, tag=None):
            name = "still%d%d" % (b, t)
            if b == 0:
                still[b, t] = ring([P, NP], F32, name, tag or name, 1)
            nc.vector.tensor_copy(still[b, t][:], h[b, t][:].indirect(pos2_t[:]))

        def pick_change(change, b, t, cols):
            lst = slice(cols.start // 16, cols.stop // 16)
            nc.vector.tensor_tensor(
                change[:, t, :], h[b, t][:].indirect(pos1_t[:, lst]), still[b, t][:, cols], ALU.subtract
            )

        def make_level(b, cols, name, last_tag="bounded"):
            width = cols.stop - cols.start
            level = ring([P, 4, width], BF16, name, "last_sums0" if b == 0 else name, 1)
            for t in range(4):
                tag = last_tag if t == 3 else "bounded"
                if b == 0:
                    tag = "bounded%d" % t
                bounded = ring([P, width], F32, "bounded", tag, 3 if tag == "bounded" else 1)
                nc.scalar.activation(
                    bounded[:], still[b, t][:, cols], ACT.Tanh, bias=zero_bias[:], scale=slope_t[:, b, t : t + 1]
                )
                if b == 0:
                    nc.gpsimd.tensor_scalar(level[:, t, :], bounded[:], gain_t[:, b, t : t + 1], 0.0, ALU.mult, ALU.add)
                else:
                    nc.scalar.activation(level[:, t, :], bounded[:], ACT.Copy, scale=gain_t[:, b, t : t + 1])
            return level

        def weave(src, name, on_vector, pieces=1, scale=None, tag=None):
            width = src.shape[2]
            grouped = grouped_tile(width, name) if tag is None else ring([P, 4 * width], BF16, name, tag, 1)
            step = width // 4 // pieces
            for x in range(pieces):
                s = src[:].rearrange("p t (c i) -> p c t i", i=4)[:, x * step : (x + 1) * step]
                d = grouped[:].rearrange("p (c i t) -> p c t i", i=4, t=4)[:, x * step : (x + 1) * step]
                if scale is not None:
                    nc.scalar.activation(d, s, ACT.Copy, scale=scale)
                elif on_vector:
                    nc.vector.tensor_copy(d, s)
                else:
                    nc.scalar.copy(d, s)
            return grouped

        accs = {(t, u): bank(2 * t + u, "acc0%d%d" % (t, u)) for t in range(4) for u in range(2)}
        for t in range(4):
            for a in range(2):
                for u in range(2):
                    first_pass(accs[t, u], a, 0, t, u)
        whole = slice(0, NP)
        late = [ring([P, 2048], BF16, "g%d1" % a, "g%d1" % a, 1) for a in range(2)]
        for a in range(2):
            round_w1((raw01, raw11)[a], late[a], 0, 0, False)
        floor_slice([accs[0, 0], accs[0, 1]], 0, 0, True)
        change_rows0 = ring([P, 4, NP], F32, "change_rows0", "change_rows0", 1)
        for t in range(4):
            if t == 1:
                for a in range(2):
                    w1q[a, 1] = quantize_w1(late[a], "w1q%d1" % a, False, ("h00", None)[a])
            pick_still(0, t, "g11" if t == 1 else None)
            if t < 3:
                floor_slice([accs[t + 1, 0], accs[t + 1, 1]], 0, t + 1, t + 1 < 3)
            pick_change(change_rows0, 0, t, whole)

        w3q = []
        for a in range(2):
            w3q.append(quantize(weave(raw3[a], "g3%d" % a, False, pieces=1, scale=-1.0), "w3q%d" % a, 1))

        for t in range(4):
            pair = [bank(2 * t + u, "acc1%d%d" % (t, u)) for u in range(2)]
            for a in range(2):
                for u in range(2):
                    first_pass(pair[u], a, 1, t, u)
            floor_slice(pair, 1, t, False)
        still1 = ring([P, 4, NP], F32, "still1", "last_sums1", 1)
        for t in range(4):
            still[1, t] = still1[:, t, :]
            pick_still(1, t)
        level_rows0 = make_level(0, whole, "level_rows0")
        change0 = quantize(weave(change_rows0, "gc0", False), "changeq0", 1)
        level0 = quantize(weave(level_rows0, "gl0", False, tag="gl0"), "levelq0", 1)

        def level_pass(acc, a, n, level, c0, width):
            rows = slice(P * n, P * (n + 1))
            nc.tensor.matmul_mx(
                out=acc[:, 0:width],
                lhsT=w3q[a][0][:, rows].bitcast(FP8X4),
                lhsT_scale=w3q[a][1][:, rows],
                rhs=level[0][:, c0 : c0 + width].bitcast(FP8X4),
                rhs_scale=level[1][:, c0 : c0 + width],
                start=(a == 0),
                stop=(a == 1),
            )

        def change_passes(acc, a, n, change, c0, width):
            for x in range(0, width, P):
                nc.tensor.matmul_mx(
                    out=acc[:, x : x + P],
                    lhsT=w2_codes[:, a, 2 * P * n : 2 * P * (n + 1)].bitcast(FP4X4),
                    lhsT_scale=w2_plane[:, N * a + P * n : N * a + P * (n + 1)],
                    rhs=change[0][:, c0 + x : c0 + x + P].bitcast(FP8X4),
                    rhs_scale=change[1][:, c0 + x : c0 + x + P],
                    start=False,
                    stop=False,
                )

        outs = {(u, n): bank(4 * u + n, "res%d%d" % (u, n)) for u in range(2) for n in range(4)}
        for u in range(2):
            for n in range(4):
                level_pass(outs[u, n], 0, n, level0, 256 * u, 256)
        for u in range(2):
            for n in range(4):
                change_passes(outs[u, n], 0, n, change0, 256 * u, 256)

        def finish(u, pieces):
            tiles_each = 4 // pieces
            for x in range(pieces):
                tag = "level_rows11" if u == 0 else "staged%d" % x
                staged = ring([P, tiles_each, 256], F32, "staged", tag, 1)
                for y in range(tiles_each):
                    nc.scalar.activation(staged[:, y, :], outs[u, tiles_each * x + y][:, 0:256], ACT.Abs)
                rows = slice(P * tiles_each * x, P * tiles_each * (x + 1))
                nc.sync.dma_start(
                    out=out[rows, 256 * u : 256 * (u + 1)].rearrange("(y p) j -> p y j", p=P), in_=staged[:]
                )

        for u in range(2):
            cols = slice(256 * u, 256 * (u + 1))
            level_rows = make_level(1, cols, "level_rows1%d" % u, "bounded")
            change_rows = ring([P, 4, 256], F32, "change_rows1%d" % u, ("change_rows0", "gl0")[u], 1)
            for t in range(4):
                pick_change(change_rows, 1, t, cols)
            if u == 0:
                level1 = quantize(weave(level_rows, "gl10", False), "levelq10", 1)
                change1 = quantize(weave(change_rows, "gc10", True, tag="last_sums0"), "changeq10", 1)
            else:
                woven = weave(change_rows, "gc11", True, tag="level_rows10"), weave(level_rows, "gl11", False)
                change1 = quantize(woven[0], "changeq11", 1)
                level1 = quantize(woven[1], "levelq11", 1)
            for n in range(4):
                change_passes(outs[u, n], 1, n, change1, 0, 256)
            for n in range(4):
                level_pass(outs[u, n], 1, n, level1, 0, 256)
        finish(0, 1)
        finish(1, 4)
